import numpy as np
import ml_dtypes


def mxq(x, axis, fmt="e4m3"):
    dtype, down = {"e4m3": (ml_dtypes.float8_e4m3fn, 7), "e5m2": (ml_dtypes.float8_e5m2, 14)}[fmt]
    v = np.moveaxis(np.asarray(x, np.float32).astype(ml_dtypes.bfloat16).astype(np.float64), axis, -1)
    blocks = v.reshape(v.shape[:-1] + (-1, 32))
    amax = np.abs(blocks).max(-1, keepdims=True)
    byte = np.maximum(np.where(amax > 0, np.frexp(amax)[1] - 1 + 127, 0) - down, 1)
    scale = np.exp2(byte - 127.0)
    codes = (blocks / scale).astype(np.float32).astype(dtype).astype(np.float64)
    return np.moveaxis((codes * scale).reshape(v.shape), -1, axis)


WIDE = False


def mx_kscale(k):
    if not WIDE:
        return np.ones(k)
    levels = np.array([30, -30])
    if k % 512:
        return np.exp2(np.random.permutation(np.resize(levels, k // 32))).repeat(32)
    a = np.empty((k // 512, 16))
    for p in range(k // 512):
        a[p, :8] = np.random.permutation(np.resize(levels, 8))
        for g in range(8):
            far = levels[np.abs(levels - a[p, g]) >= 10]
            a[p, g + 8] = far[np.random.randint(len(far))]
    return np.exp2(a.ravel()).repeat(32)


def f64(x):
    return np.asarray(x).astype(np.float64)


def striped(idx):
    return np.tile(np.asarray(idx).reshape(-1, 16).T, (8, 1)).astype(np.uint16)


def unstriped(offs):
    return offs[:16].T.reshape(-1).astype(np.int64)


E2M1 = np.array([0.0, 0.5, 1.0, 1.5, 2.0, 3.0, 4.0, 6.0, -0.0, -0.5, -1.0, -1.5, -2.0, -3.0, -4.0, -6.0])


def pack_weight(w, fmt):
    k, n = w.shape
    w = f64(np.asarray(w, np.float32).astype(ml_dtypes.bfloat16)).reshape(k // 32, 32, n)
    amax = np.abs(w).max(1)
    if fmt in ("e4m3", "e5m2"):
        byte = np.frexp(amax)[1] - 1 + 127 - (7 if fmt == "e4m3" else 14)
    else:
        mant, ex = np.frexp(amax / 6.0)
        byte = np.where(mant > 0.5, ex, ex - 1) + 127
    byte = np.clip(np.where(amax > 0, byte, 1), 1, 254)
    scaled = (w * np.exp2(127.0 - byte)[:, None, :]).reshape(k, n).astype(np.float32)
    by_word = np.ascontiguousarray(scaled.reshape(k // 512, 128, 4, n).transpose(0, 1, 3, 2))
    if fmt in ("e4m3", "e5m2"):
        words = by_word.astype(ml_dtypes.float8_e4m3fn if fmt == "e4m3" else ml_dtypes.float8_e5m2).view(np.uint8)
    else:
        c = by_word.astype(ml_dtypes.float4_e2m1fn).view(np.uint8) & 0xF
        words = (c[..., 0::2] | (c[..., 1::2] << 4)).reshape(k // 512, 128, 2 * n)
    return np.ascontiguousarray(words), np.ascontiguousarray(byte.astype(np.uint8).reshape(k // 512, 16, n))


def unpack_weight(words, scales, fmt):
    g, _, n = scales.shape
    words = np.ascontiguousarray(words).reshape(g, 128, n, -1)
    if fmt in ("e4m3", "e5m2"):
        vals = words.view(ml_dtypes.float8_e4m3fn if fmt == "e4m3" else ml_dtypes.float8_e5m2).astype(np.float64)
    else:
        nib = np.empty((g, 128, n, 4), np.uint8)
        nib[..., 0::2] = words & 0xF
        nib[..., 1::2] = words >> 4
        vals = E2M1[nib]
    vals = vals * np.repeat(np.exp2(scales.astype(np.float64) - 127.0), 8, axis=1)[..., None]
    return vals.transpose(0, 1, 3, 2).reshape(g * 512, n)


K, T, J, R, C, O, N = 1024, 1024, 256, 512, 1024, 256, 256


def setup_inputs():
    n = np.random.standard_normal
    idx = np.random.permutation(T)[:J]
    idx2 = np.random.permutation(T)[:J]
    idx3 = np.random.permutation(C)[:J]
    idx4 = np.random.permutation(C)[:O]
    fk = mx_kscale(K)
    fr = mx_kscale(R)
    wp = pack_weight(n((K, R)) * 1 / np.sqrt(K) * fk[:, None] * fr, "e5m2")
    wbp = pack_weight(n((R, N)) * 1 / np.sqrt(R) / fr[:, None], "e4m3")
    return {
        "xf": (n((K, T))).astype(np.float32),
        "fk": (np.random.uniform(0.5, 2.0, (K, 1)) / fk[:, None]).astype(np.float32),
        "w_words": wp[0],
        "w_scales": wp[1],
        "oldh": (n((R, C)) * 0.7 * fr[:, None]).astype(np.float32),
        "wb_words": wbp[0],
        "wb_scales": wbp[1],
        "rs": (1.0 * n((O, N))).astype(np.float32),
        "offs": striped(idx),
        "offs2": striped(idx2),
        "offs3": striped(idx3),
        "offs4": striped(idx4),
    }


def reference(xf, fk, w_words, w_scales, oldh, wb_words, wb_scales, rs, offs, offs2, offs3, offs4):
    idx = unstriped(offs)
    idx2 = unstriped(offs2)
    idx3 = unstriped(offs3)
    idx4 = unstriped(offs4)
    wu = unpack_weight(w_words, w_scales, "e5m2")
    wbu = unpack_weight(wb_words, wb_scales, "e4m3")
    u = (f64(xf)[:, idx] - f64(xf)[:, idx2]) * f64(fk)
    uq = mxq(u, 0, "e5m2")
    a = wu.T @ uq
    ha = np.maximum(a, 0.0)
    pw0 = np.zeros((R, C))
    pw0[:, idx3] = ha
    pg = pw0 + f64(oldh)
    hid = pg[:, idx4]
    hidq = mxq(hid, 0, "e5m2")
    p = hidq.T @ wbu
    pk2 = np.max(np.abs(p), axis=1, keepdims=True)
    y = p / (pk2 + 0.2) + 0.3 * f64(rs)
    return y

@@ -1,0 +1,175 @@
+from contextlib import ExitStack
+
+import concourse.mybir as mybir
+
+K, T, J, R, C, O, N = 1024, 1024, 256, 512, 1024, 256, 256
+FLOPS = 2 * K * R * J + 2 * R * O * N
+
+F32 = mybir.dt.float32
+BF16 = mybir.dt.bfloat16
+I32 = mybir.dt.int32
+U32 = mybir.dt.uint32
+U16 = mybir.dt.uint16
+U8 = mybir.dt.uint8
+E5M2 = mybir.dt.float8_e5m2_x4
+E4M3 = mybir.dt.float8_e4m3fn_x4
+ALU = mybir.AluOpType
+ACT = mybir.ActivationFunctionType
+
+P = 128
+PACK = 4
+PASSES = K // (P * PACK)
+LIST_COLS = J // 16
+HALVES = O // P
+
+
+def tile_list_page_pickgaps_rowpeaks_kernel(
+    tc, xf, fk, w_words, w_scales, oldh, wb_words, wb_scales, rs, offs, offs2, offs3, offs4, out
+):
+    nc = tc.nc
+    with ExitStack() as ctx:
+        keep = ctx.enter_context(tc.tile_pool(name="keep", bufs=1))
+        psum = ctx.enter_context(tc.psum_pool(name="psum", bufs=1))
+
+        def sbuf(name, shape, dtype, tag=None):
+            return keep.tile(shape, dtype, name=name, tag=tag or name, align_bytes=64)
+
+        lists = [sbuf(f"list{i}", [P, LIST_COLS], U16) for i in range(4)]
+        first, second, place, read = lists
+        x = [[sbuf(f"x{z}{t}", [P, T], F32) for t in range(PACK)] for z in range(PASSES)]
+        old = [sbuf(f"old{t}", [P, C], F32) for t in range(PACK)]
+        fresh = [sbuf(f"fresh{t}", [P, C], F32) for t in range(PACK)]
+        page = [sbuf(f"page{t}", [P, C], F32) for t in range(PACK)]
+        factor = sbuf("factor", [P, PASSES, PACK], F32)
+        w_raw = [sbuf(f"w_raw{z}", [P, R], U32) for z in range(PASSES)]
+        w_codes = [sbuf(f"w_codes{z}", [P, PACK, P], U32) for z in range(PASSES)]
+        ws_raw = sbuf("ws_raw", [P, PASSES, R], U8)
+        ws = sbuf("ws", [P, PASSES, PACK, P], U8)
+        wb_codes = sbuf("wb_codes", [P, N], U32)
+        wbs = sbuf("wbs", [P, N], U8)
+        resid = sbuf("resid", [P, HALVES, N], F32)
+
+        x_planes = xf.rearrange("(z p t) c -> z t p c", z=PASSES, t=PACK)
+        old_planes = oldh.rearrange("(p t) c -> t p c", t=PACK)
+        nc.gpsimd.memset(ws_raw[:].rearrange("p z c -> p (z c)").bitcast(U32), 0)
+        nc.gpsimd.memset(wbs[:].bitcast(U32), 0)
+        nc.sync.dma_start(second[:], offs2)
+        nc.sync.dma_start(first[:], offs)
+        nc.scalar.dma_start(factor[:], fk.rearrange("(z p t) o -> p z (t o)", z=PASSES, t=PACK))
+        for z in range(PASSES):
+            for t in range(PACK):
+                nc.sync.dma_start(x[z][t][:], x_planes[z, t])
+                if (z, t) == (0, 0):
+                    for q in range(4):
+                        nc.sync.dma_start(
+                            ws_raw[32 * q : 32 * q + 4].bitcast(I32),
+                            w_scales[:, 4 * q : 4 * q + 4, :].rearrange("z r c -> r z c").bitcast(I32),
+                        )
+            nc.sync.dma_start(w_raw[z][:].bitcast(I32), w_words[z].rearrange("p c b -> p (c b)").bitcast(I32))
+        nc.sync.dma_start(place[:], offs3)
+        nc.sync.dma_start(read[:], offs4)
+        for t in range(PACK):
+            nc.sync.dma_start(old[t][:], old_planes[t])
+        nc.sync.dma_start(wb_codes[:].bitcast(I32), wb_words[0].rearrange("p n b -> p (n b)").bitcast(I32))
+        nc.sync.dma_start(resid[:], rs.rearrange("(h p) n -> p h n", p=P))
+        for q in range(4):
+            nc.sync.dma_start(
+                wbs[32 * q : 32 * q + 4, :].bitcast(I32), wb_scales[0, 4 * q : 4 * q + 4, :].bitcast(I32)
+            )
+        for t in range(PACK):
+            nc.vector.memset(fresh[t][:], 0.0)
+
+        nc.vector.tensor_copy(
+            ws[:].rearrange("p z t m -> p z m t"), ws_raw[:].rearrange("p z (m t) -> p z m t", t=PACK)
+        )
+        acc = [psum.tile([P, J], F32, name=f"acc{t}") for t in range(PACK)]
+        for z in range(PASSES):
+            u_codes = sbuf(f"u_codes{z}", [P, J], U32)
+            u_scales = sbuf(f"u_scales{z}", [P, J], U8)
+            u_planes = sbuf(f"u_planes{z}", [P, PACK - 1, J], BF16)
+            u_woven = sbuf(f"u_woven{z}", [P, J, PACK], BF16)
+            for t in range(PACK):
+                window = x[z][t]
+                taken = sbuf(f"taken{z}{t}", [P, J], F32)
+                picked = sbuf(f"picked{z}{t}", [P, J], F32)
+                gap = sbuf(f"gap{z}{t}", [P, J], F32)
+                nc.scalar.activation(taken[:], window[:].indirect(second[:]), ACT.Copy)
+                if t == 0:
+                    nc.vector.tensor_copy(picked[:], window[:].indirect(first[:]))
+                else:
+                    nc.scalar.activation(picked[:], window[:].indirect(first[:]), ACT.Copy)
+                nc.vector.tensor_tensor(gap[:], picked[:], taken[:], ALU.subtract)
+                target = u_planes[:, t, :] if t < PACK - 1 else u_woven[:, :, t]
+                nc.vector.tensor_scalar(target, gap[:], factor[:, z, t : t + 1], None, ALU.mult)
+                if t == PACK - 2:
+                    nc.vector.tensor_copy(u_woven[:, :, 0 : PACK - 1], u_planes[:].rearrange("p t j -> p j t"))
+            nc.vector.tensor_copy(
+                w_codes[z][:].rearrange("p t m -> p m t"), w_raw[z][:].rearrange("p (m t) -> p m t", t=PACK)
+            )
+            nc.vector.quantize_mx(
+                out=u_codes[:].bitcast(E5M2), scales=u_scales[:], in_=u_woven[:].rearrange("p j t -> p (j t)")
+            )
+            for t in range(PACK):
+                nc.tensor.matmul_mx(
+                    out=acc[t][:],
+                    lhsT=w_codes[z][:, t, :].bitcast(E5M2),
+                    lhsT_scale=ws[:, z, t, :],
+                    rhs=u_codes[:].bitcast(E5M2),
+                    rhs_scale=u_scales[:],
+                    start=(z == 0),
+                    stop=(z == PASSES - 1),
+                )
+        ha = [sbuf(f"ha{t}", [P, J], F32) for t in range(PACK)]
+        nc.scalar.activation(ha[0][:], acc[0][:], ACT.Relu)
+        nc.scalar.activation(fresh[0][:].indirect(place[:]), ha[0][:], ACT.Copy)
+        nc.vector.tensor_scalar_max(ha[1][:], acc[1][:], 0.0)
+        nc.vector.tensor_scalar_max(ha[2][:], acc[2][:], 0.0)
+        nc.vector.tensor_copy(fresh[1][:].indirect(place[:]), ha[1][:])
+        nc.scalar.activation(fresh[2][:].indirect(place[:]), ha[2][:], ACT.Copy)
+        nc.scalar.activation(ha[3][:], acc[3][:], ACT.Relu)
+        nc.scalar.activation(fresh[3][:].indirect(place[:]), ha[3][:], ACT.Copy)
+
+        hid_planes = sbuf("hid_planes", [P, PACK, O], BF16)
+        half_cols = LIST_COLS // HALVES
+        for t in range(PACK):
+            nc.vector.tensor_tensor(page[t][:], fresh[t][:], old[t][:], ALU.add)
+            if t < PACK - 1:
+                nc.scalar.activation(hid_planes[:, t, :], page[t][:].indirect(read[:]), ACT.Copy)
+            else:
+                nc.vector.tensor_copy(hid_planes[:, t, 0:P], page[t][:].indirect(read[:, 0:half_cols]))
+                nc.scalar.activation(hid_planes[:, t, P:O], page[t][:].indirect(read[:, half_cols:LIST_COLS]), ACT.Copy)
+
+        hid_woven = [sbuf(f"hid_woven{h}", [P, P, PACK], BF16) for h in range(HALVES)]
+        hid_codes = [sbuf(f"hid_codes{h}", [P, P], U32) for h in range(HALVES)]
+        hid_scales = [sbuf(f"hid_scales{h}", [P, P], U8) for h in range(HALVES)]
+        nc.vector.tensor_copy(hid_woven[0][:], hid_planes[:, :, 0:P].rearrange("p t o -> p o t"))
+        nc.scalar.copy(hid_woven[1][:], hid_planes[:, :, P:O].rearrange("p t o -> p o t"))
+        resid_scaled = sbuf("resid_scaled", [P, HALVES, N], F32, tag=f"page{PACK - 1}")
+        nc.scalar.activation(resid_scaled[:], resid[:], ACT.Copy, scale=0.3)
+
+        for h in range(HALVES):
+            nc.vector.quantize_mx(
+                out=hid_codes[h][:].bitcast(E5M2),
+                scales=hid_scales[h][:],
+                in_=hid_woven[h][:].rearrange("p o t -> p (o t)"),
+            )
+        for h in range(HALVES):
+            prod = psum.tile([P, N], F32, name=f"prod{h}")
+            nc.tensor.matmul_mx(
+                out=prod[:],
+                lhsT=hid_codes[h][:].bitcast(E5M2),
+                lhsT_scale=hid_scales[h][:],
+                rhs=wb_codes[:].bitcast(E4M3),
+                rhs_scale=wbs[:],
+                start=True,
+                stop=True,
+            )
+            size = sbuf(f"size{h}", [P, N], F32)
+            denom = sbuf(f"denom{h}", [P, 1], F32)
+            inverse = sbuf(f"inverse{h}", [P, 1], F32)
+            result = sbuf(f"result{h}", [P, N], F32)
+            nc.scalar.activation(size[:], prod[:], ACT.Abs)
+            nc.vector.tensor_scalar(size[:], size[:], 0.2, None, ALU.add, ALU.max, accum_out=denom[:])
+            nc.vector.reciprocal(inverse[:], denom[:])
+            nc.vector.scalar_tensor_tensor(result[:], prod[:], inverse[:], resid_scaled[:, h, :], ALU.mult, ALU.add)
+            nc.sync.dma_start(out[h * P : (h + 1) * P, :], result[:])

@@ -53,18 +53,18 @@ def tile_list_page_pickgaps_rowpeaks_kernel(
         old_planes = oldh.rearrange("(p t) c -> t p c", t=PACK)
         nc.gpsimd.memset(ws_raw[:].rearrange("p z c -> p (z c)").bitcast(U32), 0)
         nc.gpsimd.memset(wbs[:].bitcast(U32), 0)
+        nc.sync.dma_start(x[0][0][:], x_planes[0, 0])
         nc.sync.dma_start(second[:], offs2)
         nc.sync.dma_start(first[:], offs)
         nc.scalar.dma_start(factor[:], fk.rearrange("(z p t) o -> p z (t o)", z=PASSES, t=PACK))
+        for q in range(4):
+            nc.scalar.dma_start(
+                ws_raw[32 * q : 32 * q + 4].bitcast(I32),
+                w_scales[:, 4 * q : 4 * q + 4, :].rearrange("z r c -> r z c").bitcast(I32),
+            )
+        for i in range(1, PASSES * PACK):
+            nc.sync.dma_start(x[i // PACK][i % PACK][:], x_planes[i // PACK, i % PACK])
         for z in range(PASSES):
-            for t in range(PACK):
-                nc.sync.dma_start(x[z][t][:], x_planes[z, t])
-                if (z, t) == (0, 0):
-                    for q in range(4):
-                        nc.sync.dma_start(
-                            ws_raw[32 * q : 32 * q + 4].bitcast(I32),
-                            w_scales[:, 4 * q : 4 * q + 4, :].rearrange("z r c -> r z c").bitcast(I32),
-                        )
             nc.sync.dma_start(w_raw[z][:].bitcast(I32), w_words[z].rearrange("p c b -> p (c b)").bitcast(I32))
         nc.sync.dma_start(place[:], offs3)
         nc.sync.dma_start(read[:], offs4)
@@ -80,13 +80,13 @@ def tile_list_page_pickgaps_rowpeaks_kernel(
             nc.vector.memset(fresh[t][:], 0.0)
 
         nc.vector.tensor_copy(
-            ws[:].rearrange("p z t m -> p z m t"), ws_raw[:].rearrange("p z (m t) -> p z m t", t=PACK)
+            ws[:].rearrange("p z t (a b) -> p z a t b", b=16),
+            ws_raw[:].rearrange("p z (a b t) -> p z a t b", b=16, t=PACK),
         )
         acc = [psum.tile([P, J], F32, name=f"acc{t}") for t in range(PACK)]
         for z in range(PASSES):
             u_codes = sbuf(f"u_codes{z}", [P, J], U32)
             u_scales = sbuf(f"u_scales{z}", [P, J], U8)
-            u_planes = sbuf(f"u_planes{z}", [P, PACK - 1, J], BF16)
             u_woven = sbuf(f"u_woven{z}", [P, J, PACK], BF16)
             for t in range(PACK):
                 window = x[z][t]
@@ -94,17 +94,15 @@ def tile_list_page_pickgaps_rowpeaks_kernel(
                 picked = sbuf(f"picked{z}{t}", [P, J], F32)
                 gap = sbuf(f"gap{z}{t}", [P, J], F32)
                 nc.scalar.activation(taken[:], window[:].indirect(second[:]), ACT.Copy)
-                if t == 0:
+                if t % 2 == 0:
                     nc.vector.tensor_copy(picked[:], window[:].indirect(first[:]))
                 else:
                     nc.scalar.activation(picked[:], window[:].indirect(first[:]), ACT.Copy)
                 nc.vector.tensor_tensor(gap[:], picked[:], taken[:], ALU.subtract)
-                target = u_planes[:, t, :] if t < PACK - 1 else u_woven[:, :, t]
-                nc.vector.tensor_scalar(target, gap[:], factor[:, z, t : t + 1], None, ALU.mult)
-                if t == PACK - 2:
-                    nc.vector.tensor_copy(u_woven[:, :, 0 : PACK - 1], u_planes[:].rearrange("p t j -> p j t"))
+                nc.vector.tensor_scalar(u_woven[:, :, t], gap[:], factor[:, z, t : t + 1], None, ALU.mult)
             nc.vector.tensor_copy(
-                w_codes[z][:].rearrange("p t m -> p m t"), w_raw[z][:].rearrange("p (m t) -> p m t", t=PACK)
+                w_codes[z][:].rearrange("p t (a b) -> p a t b", b=4),
+                w_raw[z][:].rearrange("p (a b t) -> p a t b", b=4, t=PACK),
             )
             nc.vector.quantize_mx(
                 out=u_codes[:].bitcast(E5M2), scales=u_scales[:], in_=u_woven[:].rearrange("p j t -> p (j t)")
@@ -124,9 +122,9 @@ def tile_list_page_pickgaps_rowpeaks_kernel(
         nc.scalar.activation(fresh[0][:].indirect(place[:]), ha[0][:], ACT.Copy)
         nc.vector.tensor_scalar_max(ha[1][:], acc[1][:], 0.0)
         nc.vector.tensor_scalar_max(ha[2][:], acc[2][:], 0.0)
+        nc.vector.tensor_scalar_max(ha[3][:], acc[3][:], 0.0)
         nc.vector.tensor_copy(fresh[1][:].indirect(place[:]), ha[1][:])
         nc.scalar.activation(fresh[2][:].indirect(place[:]), ha[2][:], ACT.Copy)
-        nc.scalar.activation(ha[3][:], acc[3][:], ACT.Relu)
         nc.scalar.activation(fresh[3][:].indirect(place[:]), ha[3][:], ACT.Copy)
 
         hid_planes = sbuf("hid_planes", [P, PACK, O], BF16)

@@ -49,6 +49,9 @@ def tile_list_page_pickgaps_rowpeaks_kernel(
         wbs = sbuf("wbs", [P, N], U8)
         resid = sbuf("resid", [P, HALVES, N], F32)
 
+        warm = sbuf("warm", [P, 2], F32)
+        nc.gpsimd.memset(warm[:, 0:1], 0.0)
+        nc.scalar.activation(warm[:, 1:2], warm[:, 0:1], ACT.Copy)
         x_planes = xf.rearrange("(z p t) c -> z t p c", z=PASSES, t=PACK)
         old_planes = oldh.rearrange("(p t) c -> t p c", t=PACK)
         nc.gpsimd.memset(ws_raw[:].rearrange("p z c -> p (z c)").bitcast(U32), 0)

from contextlib import ExitStack

import concourse.mybir as mybir

K, T, J, R, C, O, N = 1024, 1024, 256, 512, 1024, 256, 256
FLOPS = 2 * K * R * J + 2 * R * O * N

F32 = mybir.dt.float32
BF16 = mybir.dt.bfloat16
I32 = mybir.dt.int32
U32 = mybir.dt.uint32
U16 = mybir.dt.uint16
U8 = mybir.dt.uint8
E5M2 = mybir.dt.float8_e5m2_x4
E4M3 = mybir.dt.float8_e4m3fn_x4
ALU = mybir.AluOpType
ACT = mybir.ActivationFunctionType

P = 128
PACK = 4
PASSES = K // (P * PACK)
LIST_COLS = J // 16
HALVES = O // P


def tile_list_page_pickgaps_rowpeaks_kernel(
    tc, xf, fk, w_words, w_scales, oldh, wb_words, wb_scales, rs, offs, offs2, offs3, offs4, out
):
    nc = tc.nc
    with ExitStack() as ctx:
        keep = ctx.enter_context(tc.tile_pool(name="keep", bufs=1))
        psum = ctx.enter_context(tc.psum_pool(name="psum", bufs=1))

        def sbuf(name, shape, dtype, tag=None):
            return keep.tile(shape, dtype, name=name, tag=tag or name, align_bytes=64)

        lists = [sbuf(f"list{i}", [P, LIST_COLS], U16) for i in range(4)]
        first, second, place, read = lists
        x = [[sbuf(f"x{z}{t}", [P, T], F32) for t in range(PACK)] for z in range(PASSES)]
        old = [sbuf(f"old{t}", [P, C], F32) for t in range(PACK)]
        fresh = [sbuf(f"fresh{t}", [P, C], F32) for t in range(PACK)]
        page = [sbuf(f"page{t}", [P, C], F32) for t in range(PACK)]
        factor = sbuf("factor", [P, PASSES, PACK], F32)
        w_raw = [sbuf(f"w_raw{z}", [P, R], U32) for z in range(PASSES)]
        w_codes = [sbuf(f"w_codes{z}", [P, PACK, P], U32) for z in range(PASSES)]
        ws_raw = sbuf("ws_raw", [P, PASSES, R], U8)
        ws = sbuf("ws", [P, PASSES, PACK, P], U8)
        wb_codes = sbuf("wb_codes", [P, N], U32)
        wbs = sbuf("wbs", [P, N], U8)
        resid = sbuf("resid", [P, HALVES, N], F32)

        warm = sbuf("warm", [P, 2], F32)
        nc.gpsimd.memset(warm[:, 0:1], 0.0)
        nc.scalar.activation(warm[:, 1:2], warm[:, 0:1], ACT.Copy)
        x_planes = xf.rearrange("(z p t) c -> z t p c", z=PASSES, t=PACK)
        old_planes = oldh.rearrange("(p t) c -> t p c", t=PACK)
        nc.gpsimd.memset(ws_raw[:].rearrange("p z c -> p (z c)").bitcast(U32), 0)
        nc.gpsimd.memset(wbs[:].bitcast(U32), 0)
        nc.sync.dma_start(x[0][0][:], x_planes[0, 0])
        nc.sync.dma_start(second[:], offs2)
        nc.sync.dma_start(first[:], offs)
        nc.scalar.dma_start(factor[:], fk.rearrange("(z p t) o -> p z (t o)", z=PASSES, t=PACK))
        for q in range(4):
            nc.scalar.dma_start(
                ws_raw[32 * q : 32 * q + 4].bitcast(I32),
                w_scales[:, 4 * q : 4 * q + 4, :].rearrange("z r c -> r z c").bitcast(I32),
            )
        for i in range(1, PASSES * PACK):
            nc.sync.dma_start(x[i // PACK][i % PACK][:], x_planes[i // PACK, i % PACK])
        for z in range(PASSES):
            nc.sync.dma_start(w_raw[z][:].bitcast(I32), w_words[z].rearrange("p c b -> p (c b)").bitcast(I32))
        nc.sync.dma_start(place[:], offs3)
        nc.sync.dma_start(read[:], offs4)
        for t in range(PACK):
            nc.sync.dma_start(old[t][:], old_planes[t])
        nc.sync.dma_start(wb_codes[:].bitcast(I32), wb_words[0].rearrange("p n b -> p (n b)").bitcast(I32))
        nc.sync.dma_start(resid[:], rs.rearrange("(h p) n -> p h n", p=P))
        for q in range(4):
            nc.sync.dma_start(
                wbs[32 * q : 32 * q + 4, :].bitcast(I32), wb_scales[0, 4 * q : 4 * q + 4, :].bitcast(I32)
            )
        for t in range(PACK):
            nc.vector.memset(fresh[t][:], 0.0)

        nc.vector.tensor_copy(
            ws[:].rearrange("p z t (a b) -> p z a t b", b=16),
            ws_raw[:].rearrange("p z (a b t) -> p z a t b", b=16, t=PACK),
        )
        acc = [psum.tile([P, J], F32, name=f"acc{t}") for t in range(PACK)]
        for z in range(PASSES):
            u_codes = sbuf(f"u_codes{z}", [P, J], U32)
            u_scales = sbuf(f"u_scales{z}", [P, J], U8)
            u_woven = sbuf(f"u_woven{z}", [P, J, PACK], BF16)
            for t in range(PACK):
                window = x[z][t]
                taken = sbuf(f"taken{z}{t}", [P, J], F32)
                picked = sbuf(f"picked{z}{t}", [P, J], F32)
                gap = sbuf(f"gap{z}{t}", [P, J], F32)
                nc.scalar.activation(taken[:], window[:].indirect(second[:]), ACT.Copy)
                if t % 2 == 0:
                    nc.vector.tensor_copy(picked[:], window[:].indirect(first[:]))
                else:
                    nc.scalar.activation(picked[:], window[:].indirect(first[:]), ACT.Copy)
                nc.vector.tensor_tensor(gap[:], picked[:], taken[:], ALU.subtract)
                nc.vector.tensor_scalar(u_woven[:, :, t], gap[:], factor[:, z, t : t + 1], None, ALU.mult)
            nc.vector.tensor_copy(
                w_codes[z][:].rearrange("p t (a b) -> p a t b", b=4),
                w_raw[z][:].rearrange("p (a b t) -> p a t b", b=4, t=PACK),
            )
            nc.vector.quantize_mx(
                out=u_codes[:].bitcast(E5M2), scales=u_scales[:], in_=u_woven[:].rearrange("p j t -> p (j t)")
            )
            for t in range(PACK):
                nc.tensor.matmul_mx(
                    out=acc[t][:],
                    lhsT=w_codes[z][:, t, :].bitcast(E5M2),
                    lhsT_scale=ws[:, z, t, :],
                    rhs=u_codes[:].bitcast(E5M2),
                    rhs_scale=u_scales[:],
                    start=(z == 0),
                    stop=(z == PASSES - 1),
                )
        ha = [sbuf(f"ha{t}", [P, J], F32) for t in range(PACK)]
        nc.scalar.activation(ha[0][:], acc[0][:], ACT.Relu)
        nc.scalar.activation(fresh[0][:].indirect(place[:]), ha[0][:], ACT.Copy)
        nc.vector.tensor_scalar_max(ha[1][:], acc[1][:], 0.0)
        nc.vector.tensor_scalar_max(ha[2][:], acc[2][:], 0.0)
        nc.vector.tensor_scalar_max(ha[3][:], acc[3][:], 0.0)
        nc.vector.tensor_copy(fresh[1][:].indirect(place[:]), ha[1][:])
        nc.scalar.activation(fresh[2][:].indirect(place[:]), ha[2][:], ACT.Copy)
        nc.scalar.activation(fresh[3][:].indirect(place[:]), ha[3][:], ACT.Copy)

        hid_planes = sbuf("hid_planes", [P, PACK, O], BF16)
        half_cols = LIST_COLS // HALVES
        for t in range(PACK):
            nc.vector.tensor_tensor(page[t][:], fresh[t][:], old[t][:], ALU.add)
            if t < PACK - 1:
                nc.scalar.activation(hid_planes[:, t, :], page[t][:].indirect(read[:]), ACT.Copy)
            else:
                nc.vector.tensor_copy(hid_planes[:, t, 0:P], page[t][:].indirect(read[:, 0:half_cols]))
                nc.scalar.activation(hid_planes[:, t, P:O], page[t][:].indirect(read[:, half_cols:LIST_COLS]), ACT.Copy)

        hid_woven = [sbuf(f"hid_woven{h}", [P, P, PACK], BF16) for h in range(HALVES)]
        hid_codes = [sbuf(f"hid_codes{h}", [P, P], U32) for h in range(HALVES)]
        hid_scales = [sbuf(f"hid_scales{h}", [P, P], U8) for h in range(HALVES)]
        nc.vector.tensor_copy(hid_woven[0][:], hid_planes[:, :, 0:P].rearrange("p t o -> p o t"))
        nc.scalar.copy(hid_woven[1][:], hid_planes[:, :, P:O].rearrange("p t o -> p o t"))
        resid_scaled = sbuf("resid_scaled", [P, HALVES, N], F32, tag=f"page{PACK - 1}")
        nc.scalar.activation(resid_scaled[:], resid[:], ACT.Copy, scale=0.3)

        for h in range(HALVES):
            nc.vector.quantize_mx(
                out=hid_codes[h][:].bitcast(E5M2),
                scales=hid_scales[h][:],
                in_=hid_woven[h][:].rearrange("p o t -> p (o t)"),
            )
        for h in range(HALVES):
            prod = psum.tile([P, N], F32, name=f"prod{h}")
            nc.tensor.matmul_mx(
                out=prod[:],
                lhsT=hid_codes[h][:].bitcast(E5M2),
                lhsT_scale=hid_scales[h][:],
                rhs=wb_codes[:].bitcast(E4M3),
                rhs_scale=wbs[:],
                start=True,
                stop=True,
            )
            size = sbuf(f"size{h}", [P, N], F32)
            denom = sbuf(f"denom{h}", [P, 1], F32)
            inverse = sbuf(f"inverse{h}", [P, 1], F32)
            result = sbuf(f"result{h}", [P, N], F32)
            nc.scalar.activation(size[:], prod[:], ACT.Abs)
            nc.vector.tensor_scalar(size[:], size[:], 0.2, None, ALU.add, ALU.max, accum_out=denom[:])
            nc.vector.reciprocal(inverse[:], denom[:])
            nc.vector.scalar_tensor_tensor(result[:], prod[:], inverse[:], resid_scaled[:, h, :], ALU.mult, ALU.add)
            nc.sync.dma_start(out[h * P : (h + 1) * P, :], result[:])
